import numpy as np
import ml_dtypes


def mxq(x, axis, fmt="e4m3"):
    dtype, down = {"e4m3": (ml_dtypes.float8_e4m3fn, 7), "e5m2": (ml_dtypes.float8_e5m2, 14)}[fmt]
    v = np.moveaxis(np.asarray(x, np.float32).astype(ml_dtypes.bfloat16).astype(np.float64), axis, -1)
    blocks = v.reshape(v.shape[:-1] + (-1, 32))
    amax = np.abs(blocks).max(-1, keepdims=True)
    byte = np.maximum(np.where(amax > 0, np.frexp(amax)[1] - 1 + 127, 0) - down, 1)
    scale = np.exp2(byte - 127.0)
    codes = (blocks / scale).astype(np.float32).astype(dtype).astype(np.float64)
    return np.moveaxis((codes * scale).reshape(v.shape), -1, axis)


WIDE = False


def mx_kscale(k):
    if not WIDE:
        return np.ones(k)
    levels = np.array([24, -24, 12, -12, 0])
    if k % 512:
        return np.exp2(np.random.permutation(np.resize(levels, k // 32))).repeat(32)
    a = np.empty((k // 512, 16))
    for p in range(k // 512):
        a[p, :8] = np.random.permutation(np.resize(levels, 8))
        for g in range(8):
            far = levels[np.abs(levels - a[p, g]) >= 10]
            a[p, g + 8] = far[np.random.randint(len(far))]
    return np.exp2(a.ravel()).repeat(32)


def f64(x):
    return np.asarray(x).astype(np.float64)


def striped(idx):
    return np.tile(idx.reshape(-1, 16).T, (8, 1)).astype(np.uint16)


def unstriped(offs):
    return offs[:16].T.reshape(-1).astype(np.int64)


E2M1 = np.array([0.0, 0.5, 1.0, 1.5, 2.0, 3.0, 4.0, 6.0, -0.0, -0.5, -1.0, -1.5, -2.0, -3.0, -4.0, -6.0])


def pack_weight(w, fmt):
    k, n = w.shape
    w = f64(np.asarray(w, np.float32).astype(ml_dtypes.bfloat16)).reshape(k // 32, 32, n)
    amax = np.abs(w).max(1)
    if fmt == "e4m3":
        byte = np.frexp(amax)[1] - 1 + 127 - 7
    else:
        mant, ex = np.frexp(amax / 6.0)
        byte = np.where(mant > 0.5, ex, ex - 1) + 127
    byte = np.clip(np.where(amax > 0, byte, 1), 1, 254)
    scaled = (w * np.exp2(127.0 - byte)[:, None, :]).reshape(k, n).astype(np.float32)
    by_word = np.ascontiguousarray(scaled.reshape(k // 512, 128, 4, n).transpose(0, 1, 3, 2))
    if fmt == "e4m3":
        words = by_word.astype(ml_dtypes.float8_e4m3fn).view(np.uint8)
    else:
        c = by_word.astype(ml_dtypes.float4_e2m1fn).view(np.uint8) & 0xF
        words = (c[..., 0::2] | (c[..., 1::2] << 4)).reshape(k // 512, 128, 2 * n)
    return np.ascontiguousarray(words), np.ascontiguousarray(byte.astype(np.uint8).reshape(k // 512, 16, n))


def unpack_weight(words, scales, fmt):
    g, _, n = scales.shape
    words = np.ascontiguousarray(words).reshape(g, 128, n, -1)
    if fmt == "e4m3":
        vals = words.view(ml_dtypes.float8_e4m3fn).astype(np.float64)
    else:
        nib = np.empty((g, 128, n, 4), np.uint8)
        nib[..., 0::2] = words & 0xF
        nib[..., 1::2] = words >> 4
        vals = E2M1[nib]
    vals = vals * np.repeat(np.exp2(scales.astype(np.float64) - 127.0), 8, axis=1)[..., None]
    return vals.transpose(0, 1, 3, 2).reshape(g * 512, n)


def pack_table4(v):
    words, scales = pack_weight(v, "e2m1")
    g, t = words.shape[0] // 2, v.shape[1]
    return np.ascontiguousarray(words.reshape(g, 2, 128, t, 2).transpose(0, 2, 3, 1, 4).reshape(g, 128, t, 4)), scales


def unpack_table4(words, scales):
    g, _, t, _ = words.shape
    return unpack_weight(words.reshape(g, 128, t, 2, 2).transpose(0, 3, 1, 2, 4).reshape(2 * g, 128, 2 * t), scales, "e2m1")


def planes(y):
    n, m = y.shape
    v = y.astype(np.float32).astype(ml_dtypes.bfloat16).astype(np.float64).reshape(n // 32, 32, m)
    top = np.abs(v).max(1)
    byte = np.clip(np.where(top > 0, np.frexp(top)[1] - 1 + 127 - 7, 1), 1, 254)
    codes = (v * np.exp2(127.0 - byte)[:, None, :]).reshape(n, m).astype(np.float32).astype(ml_dtypes.float8_e4m3fn).view(np.uint8)
    words = codes.reshape(n // 512, 128, 4, m).transpose(0, 1, 3, 2)
    return np.ascontiguousarray(words), np.ascontiguousarray(byte.astype(np.uint8).reshape(n // 512, 16, m))


def sigm(f):
    return 1.0 / (1.0 + np.exp(-np.maximum(f, -700.0)))


K, N, T, J = 1024, 512, 2048, 1024


def setup_inputs():
    n = np.random.standard_normal
    s = mx_kscale(K)[:, None]
    wv = n((K, N)) / np.sqrt(K) / s
    p_tab = pack_table4(n((K, T)) * s)
    p_wk = pack_weight(n((K, N)) / np.sqrt(K) / s, "e2m1")
    p_wv4 = pack_weight(wv[512:], "e2m1")
    return {
        "tab_words": p_tab[0],
        "tab_scales": p_tab[1],
        "wk_words": p_wk[0],
        "wk_scales": p_wk[1],
        "wv8": (wv[:512]).astype(np.float32),
        "wv4_words": p_wv4[0],
        "wv4_scales": p_wv4[1],
        "st": (n((N, J))).astype(np.float32),
        "rT": (n((N, T))).astype(np.float32),
        "offs": striped(np.random.permutation(T)[:J]),
    }


def reference(tab_words, tab_scales, wk_words, wk_scales, wv8, wv4_words, wv4_scales, st, rT, offs):
    idx = unstriped(offs)
    tab_ = unpack_table4(tab_words, tab_scales)[:, idx]
    wk_ = unpack_weight(wk_words, wk_scales, "e2m1")
    wv8_ = mxq(f64(wv8), 0, "e4m3")
    wv4_ = unpack_weight(wv4_words, wv4_scales, "e2m1")
    ke = wk_.T @ tab_
    ve = wv8_.T @ tab_[:512] + wv4_.T @ tab_[512:]
    gate = sigm(ke * f64(st))
    out_0 = f64(rT)[:, idx] + gate * ve
    return (out_0,) + planes(out_0)

@@ -1,0 +1,218 @@
+from contextlib import ExitStack
+
+import concourse.mybir as mybir
+
+K, N, T, J = 1024, 512, 2048, 1024
+FLOPS = 2 * 2 * K * N * J
+
+F32 = mybir.dt.float32
+BF16 = mybir.dt.bfloat16
+I32 = mybir.dt.int32
+U32 = mybir.dt.uint32
+U16 = mybir.dt.uint16
+U8 = mybir.dt.uint8
+FP8X4 = mybir.dt.float8_e4m3fn_x4
+FP4X4 = mybir.dt.float4_e2m1fn_x4
+MULT = mybir.AluOpType.mult
+ADD = mybir.AluOpType.add
+SIGMOID = mybir.ActivationFunctionType.Sigmoid
+
+P = 128
+PACK = 4
+HALF = 512
+LIST_ROWS = 16
+PIECES = ((0, 256), (256, 256), (512, 256), (768, 128), (896, 128))
+
+
+def tile_list_engram_qf_sigLP_kernel(
+    tc, tab_words, tab_scales, wk_words, wk_scales, wv8, wv4_words, wv4_scales, st, rT, offs, out_0, out_1, out_2
+):
+    nc = tc.nc
+    with ExitStack() as ctx:
+        held = ctx.enter_context(tc.tile_pool(name="held", bufs=1))
+        ring = ctx.enter_context(tc.tile_pool(name="ring", bufs=8))
+        psum = ctx.enter_context(tc.psum_pool(name="psum", bufs=1))
+
+        offsets = held.tile([P, J // LIST_ROWS], U16, name="offsets")
+        nc.sync.dma_start(offsets[:], offs)
+
+        def listed(j0, width):
+            return offsets[:, j0 // LIST_ROWS : (j0 + width) // LIST_ROWS]
+
+        tab_plane = held.tile([P, T], U8, name="tab_plane", align_bytes=64)
+        nc.vector.memset(tab_plane[:].bitcast(I32), 0)
+        w_plane_raw = held.tile([P, 3, N], U8, name="w_plane_raw", align_bytes=64)
+        nc.gpsimd.memset(w_plane_raw[:].rearrange("p i n -> p (i n)").bitcast(I32), 0)
+
+        v_plane = [held.tile([P, J], U8, name="v_plane%d" % a, align_bytes=64) for a in range(2)]
+        nc.gpsimd.memset(v_plane[1][:].bitcast(I32), 0)
+
+        w_words_raw = [held.tile([P, 2 * N], U8, name="w_words_raw%d" % i, align_bytes=64) for i in range(3)]
+        for i, src in enumerate((wk_words[0], wk_words[1], wv4_words[0])):
+            nc.sync.dma_start(w_words_raw[i][:].bitcast(I32), src.bitcast(I32))
+
+        for q in range(4):
+            nc.sync.dma_start(
+                tab_plane[32 * q : 32 * q + 8, :].bitcast(I32),
+                tab_scales[:, 4 * q : 4 * q + 4, :].bitcast(I32),
+            )
+        tab = held.tile([P, T], I32, name="tab", tag="big1", align_bytes=64)
+        nc.sync.dma_start(tab[:], tab_words[0].rearrange("p t b -> p (t b)").bitcast(I32))
+
+        for q in range(4):
+            nc.sync.dma_start(
+                w_plane_raw[32 * q : 32 * q + 4, 0:2, :].bitcast(I32),
+                wk_scales[:, 4 * q : 4 * q + 4, :].rearrange("a r n -> r a n").bitcast(I32),
+            )
+        for q in range(4):
+            nc.sync.dma_start(
+                w_plane_raw[32 * q : 32 * q + 4, 2, :].bitcast(I32),
+                wv4_scales[0, 4 * q : 4 * q + 4, :].bitcast(I32),
+            )
+
+        wv8_raw = held.tile([P, PACK, N], F32, name="wv8_raw", tag="big2", align_bytes=64)
+        nc.sync.dma_start(wv8_raw[:], wv8.rearrange("(p i) n -> p i n", i=PACK))
+
+        st_rows = st.rearrange("(p t) j -> p t j", t=PACK)
+        r_rows = rT.rearrange("(p t) c -> p t c", t=PACK)
+        y_rows = out_0.rearrange("(p t) j -> p t j", t=PACK)
+        state = [
+            held.tile([P, PACK, HALF], F32, name="state%d" % h, tag=("big3", "big4")[h], align_bytes=64)
+            for h in range(2)
+        ]
+        for h in range(2):
+            nc.sync.dma_start(state[h][:], st_rows[:, :, h * HALF : (h + 1) * HALF])
+        record = []
+
+        def load_record(t):
+            r = held.tile([P, T], F32, name="record%d" % t, tag="big%d" % t, align_bytes=64)
+            nc.sync.dma_start(r[:], r_rows[:, t, :])
+            record.append(r)
+
+        load_record(0)
+
+        w_words = [held.tile([P, 2 * N], U8, name="w_words%d" % i, align_bytes=64) for i in range(3)]
+        for i in range(3):
+            nc.vector.tensor_copy(
+                w_words[i][:].bitcast(U16).rearrange("p (t m) -> p t m", t=PACK),
+                w_words_raw[i][:].bitcast(U16).rearrange("p (m t) -> p t m", t=PACK),
+            )
+
+        nc.vector.tensor_copy(v_plane[0][:], tab_plane[:].indirect(offsets[:]))
+        for q in range(4):
+            nc.scalar.dma_start(
+                v_plane[1][32 * q : 32 * q + 4, :].bitcast(I32), v_plane[0][32 * q + 4 : 32 * q + 8, :].bitcast(I32)
+            )
+
+        v_words = []
+        picked = []
+        for h in range(2):
+            g = held.tile([P, HALF], U32, name="picked%d" % h, align_bytes=64)
+            nc.vector.tensor_copy(g[:], tab[:].bitcast(U32).indirect(listed(h * HALF, HALF)))
+            picked.append(g)
+            if h == 0:
+                w_plane = held.tile([P, 3, N], U8, name="w_plane", align_bytes=64)
+                nc.vector.tensor_copy(
+                    w_plane[:].rearrange("p i (t m) -> p i t m", t=PACK),
+                    w_plane_raw[:].rearrange("p i (m t) -> p i t m", t=PACK),
+                )
+            parted = held.tile([P, 2, 2 * HALF], U8, name="v_words%d" % h, align_bytes=64)
+            nc.vector.tensor_copy(
+                parted[:].bitcast(U16),
+                picked[h][:].bitcast(U16).rearrange("p (j d) -> p d j", d=2),
+            )
+            v_words.append(parted)
+
+        load_record(1)
+        wv8_b = held.tile([P, PACK * N], BF16, name="wv8_b", align_bytes=64)
+        nc.scalar.copy(
+            wv8_b[:].rearrange("p (t m i) -> p m t i", t=PACK, i=PACK),
+            wv8_raw[:].rearrange("p i (m t) -> p m t i", t=PACK),
+        )
+        load_record(2)
+        wv8_codes = held.tile([P, N], U32, name="wv8_codes", align_bytes=64)
+        wv8_plane = held.tile([P, N], U8, name="wv8_plane", align_bytes=64)
+
+        def fp4_weight(i, t):
+            return w_words[i][:, 2 * P * t : 2 * P * (t + 1)].bitcast(FP4X4), w_plane[:, i, P * t : P * (t + 1)]
+
+        def product(bank, weights, h):
+            for a, (w, s) in enumerate(weights):
+                nc.tensor.matmul_mx(
+                    out=bank[:],
+                    lhsT=w,
+                    lhsT_scale=s,
+                    rhs=v_words[h][:, a, :].bitcast(FP4X4),
+                    rhs_scale=v_plane[a][:, h * HALF : (h + 1) * HALF],
+                    start=(a == 0),
+                    stop=(a == 1),
+                )
+
+        gated = [held.tile([P, J], F32, name="gated%d" % t) for t in range(PACK)]
+
+        def gates(h):
+            out = []
+            for t in range(PACK):
+                ke = psum.tile([P, HALF], F32, name="ke%d" % t)
+                product(ke, (fp4_weight(0, t), fp4_weight(1, t)), h)
+                z = ring.tile([P, HALF], F32, name="z")
+                nc.vector.tensor_tensor(z[:], ke[:], state[h][:, t, :], MULT)
+                gate = ring.tile([P, HALF], F32, name="gate")
+                nc.scalar.activation(gate[:], z[:], SIGMOID)
+                out.append(gate)
+            return out
+
+        def values(h, gate):
+            for t in range(PACK):
+                ve = psum.tile([P, HALF], F32, name="ve%d" % t)
+                w8 = (wv8_codes[:, P * t : P * (t + 1)].bitcast(FP8X4), wv8_plane[:, P * t : P * (t + 1)])
+                product(ve, (w8, fp4_weight(2, t)), h)
+                nc.vector.tensor_tensor(gated[t][:, h * HALF : (h + 1) * HALF], ve[:], gate[t][:], MULT)
+
+        y_plane = held.tile([P, J], U8, name="y_plane", align_bytes=64)
+        y_codes = held.tile([P, J], U32, name="y_codes", align_bytes=64)
+        out_words = out_1[0].rearrange("p j b -> p (j b)").bitcast(I32)
+
+        gate0 = gates(0)
+        load_record(3)
+        nc.vector.quantize_mx(out=wv8_codes[:].bitcast(FP8X4), scales=wv8_plane[:], in_=wv8_b[:])
+        gate1 = gates(1)
+        values(0, gate0)
+        values(1, gate1)
+
+        rounded = [held.tile([P, width, PACK], BF16, name="yb%d" % j0, align_bytes=64) for j0, width in PIECES]
+        y01 = held.tile([P, 2, J], F32, name="y01")
+        for t in range(2):
+            nc.vector.tensor_tensor(y01[:, t, :], record[t][:].indirect(offsets[:]), gated[t][:], ADD)
+            nc.sync.dma_start(y_rows[:, t, :], y01[:, t, :])
+        for (j0, width), yb in zip(PIECES, rounded):
+            nc.scalar.copy(yb[:, :, 0:2], y01[:, :, j0 : j0 + width].rearrange("p t j -> p j t"))
+
+        def add_records(j0, width, yb):
+            y23 = held.tile([P, 2, width], F32, name="y23_%d" % j0)
+            for t in (2, 3):
+                nc.vector.tensor_tensor(
+                    y23[:, t - 2, :], record[t][:].indirect(listed(j0, width)), gated[t][:, j0 : j0 + width], ADD
+                )
+            nc.sync.dma_start(y_rows[:, 2:4, j0 : j0 + width], y23[:])
+            nc.scalar.copy(yb[:, :, 2:4], y23[:].rearrange("p t j -> p j t"))
+
+        def quantise(j0, width, yb):
+            nc.vector.quantize_mx(
+                out=y_codes[:, j0 : j0 + width].bitcast(FP8X4),
+                scales=y_plane[:, j0 : j0 + width],
+                in_=yb[:].rearrange("p j t -> p (j t)"),
+            )
+
+        for i, (j0, width) in enumerate(PIECES):
+            add_records(j0, width, rounded[i])
+            if i > 0:
+                quantise(*PIECES[i - 1], rounded[i - 1])
+            if i == 3:
+                nc.sync.dma_start(out_words[:, 0:j0], y_codes[:, 0:j0].bitcast(I32))
+        quantise(*PIECES[-1], rounded[-1])
+        nc.sync.dma_start(out_words[:, PIECES[3][0] : J], y_codes[:, PIECES[3][0] : J].bitcast(I32))
+        for q in range(4):
+            nc.scalar.dma_start(
+                out_2[0, 4 * q : 4 * q + 4, :].bitcast(I32), y_plane[32 * q : 32 * q + 4, :].bitcast(I32)
+            )

@@ -41,15 +41,18 @@ def tile_list_engram_qf_sigLP_kernel(
 
         tab_plane = held.tile([P, T], U8, name="tab_plane", align_bytes=64)
         nc.vector.memset(tab_plane[:].bitcast(I32), 0)
-        w_plane_raw = held.tile([P, 3, N], U8, name="w_plane_raw", align_bytes=64)
-        nc.gpsimd.memset(w_plane_raw[:].rearrange("p i n -> p (i n)").bitcast(I32), 0)
+        wk_plane_raw = held.tile([P, 2, N], U8, name="wk_plane_raw", tag="picked1", align_bytes=64)
+        nc.gpsimd.memset(wk_plane_raw[:].rearrange("p i n -> p (i n)").bitcast(I32), 0)
+        wv4_plane_raw = held.tile([P, N], U8, name="wv4_plane_raw", align_bytes=64)
+        nc.gpsimd.memset(wv4_plane_raw[:].bitcast(I32), 0)
 
         v_plane = [held.tile([P, J], U8, name="v_plane%d" % a, align_bytes=64) for a in range(2)]
         nc.gpsimd.memset(v_plane[1][:].bitcast(I32), 0)
 
-        w_words_raw = [held.tile([P, 2 * N], U8, name="w_words_raw%d" % i, align_bytes=64) for i in range(3)]
-        for i, src in enumerate((wk_words[0], wk_words[1], wv4_words[0])):
-            nc.sync.dma_start(w_words_raw[i][:].bitcast(I32), src.bitcast(I32))
+        wk_raw = held.tile([P, 2, 2 * N], U8, name="wk_raw", align_bytes=64)
+        nc.sync.dma_start(wk_raw[:].bitcast(I32), wk_words.rearrange("a p b -> p a b").bitcast(I32))
+        wv4_raw = held.tile([P, 2 * N], U8, name="wv4_raw", align_bytes=64)
+        nc.sync.dma_start(wv4_raw[:].bitcast(I32), wv4_words[0].bitcast(I32))
 
         for q in range(4):
             nc.sync.dma_start(
@@ -58,20 +61,19 @@ def tile_list_engram_qf_sigLP_kernel(
             )
         tab = held.tile([P, T], I32, name="tab", tag="big1", align_bytes=64)
         nc.sync.dma_start(tab[:], tab_words[0].rearrange("p t b -> p (t b)").bitcast(I32))
+        wv8_raw = held.tile([P, PACK, N], F32, name="wv8_raw", tag="big2", align_bytes=64)
+        nc.sync.dma_start(wv8_raw[:], wv8.rearrange("(p i) n -> p i n", i=PACK))
 
         for q in range(4):
-            nc.sync.dma_start(
-                w_plane_raw[32 * q : 32 * q + 4, 0:2, :].bitcast(I32),
+            nc.gpsimd.dma_start(
+                wk_plane_raw[32 * q : 32 * q + 4, :, :].bitcast(I32),
                 wk_scales[:, 4 * q : 4 * q + 4, :].rearrange("a r n -> r a n").bitcast(I32),
             )
         for q in range(4):
-            nc.sync.dma_start(
-                w_plane_raw[32 * q : 32 * q + 4, 2, :].bitcast(I32),
+            nc.gpsimd.dma_start(
+                wv4_plane_raw[32 * q : 32 * q + 4, :].bitcast(I32),
                 wv4_scales[0, 4 * q : 4 * q + 4, :].bitcast(I32),
             )
-
-        wv8_raw = held.tile([P, PACK, N], F32, name="wv8_raw", tag="big2", align_bytes=64)
-        nc.sync.dma_start(wv8_raw[:], wv8.rearrange("(p i) n -> p i n", i=PACK))
 
         st_rows = st.rearrange("(p t) j -> p t j", t=PACK)
         r_rows = rT.rearrange("(p t) c -> p t c", t=PACK)
@@ -89,14 +91,17 @@ def tile_list_engram_qf_sigLP_kernel(
             nc.sync.dma_start(r[:], r_rows[:, t, :])
             record.append(r)
 
-        load_record(0)
-
-        w_words = [held.tile([P, 2 * N], U8, name="w_words%d" % i, align_bytes=64) for i in range(3)]
-        for i in range(3):
-            nc.vector.tensor_copy(
-                w_words[i][:].bitcast(U16).rearrange("p (t m) -> p t m", t=PACK),
-                w_words_raw[i][:].bitcast(U16).rearrange("p (m t) -> p t m", t=PACK),
-            )
+        wk_w = held.tile([P, 2, 2 * N], U8, name="wk_w", align_bytes=64)
+        nc.vector.tensor_copy(
+            wk_w[:].bitcast(U16).rearrange("p a (t m) -> p a t m", t=PACK),
+            wk_raw[:].bitcast(U16).rearrange("p a (m t) -> p a t m", t=PACK),
+        )
+        wv4_w = held.tile([P, 2 * N], U8, name="wv4_w", align_bytes=64)
+        nc.vector.tensor_copy(
+            wv4_w[:].bitcast(U16).rearrange("p (t m) -> p t m", t=PACK),
+            wv4_raw[:].bitcast(U16).rearrange("p (m t) -> p t m", t=PACK),
+        )
+        w_words = (wk_w[:, 0, :], wk_w[:, 1, :], wv4_w[:])
 
         nc.vector.tensor_copy(v_plane[0][:], tab_plane[:].indirect(offsets[:]))
         for q in range(4):
@@ -104,24 +109,27 @@ def tile_list_engram_qf_sigLP_kernel(
                 v_plane[1][32 * q : 32 * q + 4, :].bitcast(I32), v_plane[0][32 * q + 4 : 32 * q + 8, :].bitcast(I32)
             )
 
-        v_words = []
-        picked = []
-        for h in range(2):
-            g = held.tile([P, HALF], U32, name="picked%d" % h, align_bytes=64)
-            nc.vector.tensor_copy(g[:], tab[:].bitcast(U32).indirect(listed(h * HALF, HALF)))
-            picked.append(g)
-            if h == 0:
-                w_plane = held.tile([P, 3, N], U8, name="w_plane", align_bytes=64)
-                nc.vector.tensor_copy(
-                    w_plane[:].rearrange("p i (t m) -> p i t m", t=PACK),
-                    w_plane_raw[:].rearrange("p i (m t) -> p i t m", t=PACK),
-                )
+        load_record(0)
+        def pick_words(h):
+            picked = held.tile([P, HALF], U32, name="picked%d" % h, tag="picked%d" % h, align_bytes=64)
+            nc.vector.tensor_copy(picked[:], tab[:].bitcast(U32).indirect(listed(h * HALF, HALF)))
             parted = held.tile([P, 2, 2 * HALF], U8, name="v_words%d" % h, align_bytes=64)
-            nc.vector.tensor_copy(
-                parted[:].bitcast(U16),
-                picked[h][:].bitcast(U16).rearrange("p (j d) -> p d j", d=2),
-            )
-            v_words.append(parted)
+            nc.vector.tensor_copy(parted[:].bitcast(U16), picked[:].bitcast(U16).rearrange("p (j d) -> p d j", d=2))
+            return parted
+
+        v_words = [pick_words(0)]
+        wk_plane = held.tile([P, 2, N], U8, name="wk_plane", tag="picked0", align_bytes=64)
+        nc.vector.tensor_copy(
+            wk_plane[:].rearrange("p a (t m) -> p a t m", t=PACK),
+            wk_plane_raw[:].rearrange("p a (m t) -> p a t m", t=PACK),
+        )
+        v_words.append(pick_words(1))
+        wv4_plane = held.tile([P, N], U8, name="wv4_plane", align_bytes=64)
+        nc.gpsimd.tensor_copy(
+            wv4_plane[:].rearrange("p (t m) -> p t m", t=PACK),
+            wv4_plane_raw[:].rearrange("p (m t) -> p t m", t=PACK),
+        )
+        w_planes = (wk_plane[:, 0, :], wk_plane[:, 1, :], wv4_plane[:])
 
         load_record(1)
         wv8_b = held.tile([P, PACK * N], BF16, name="wv8_b", align_bytes=64)
@@ -134,7 +142,7 @@ def tile_list_engram_qf_sigLP_kernel(
         wv8_plane = held.tile([P, N], U8, name="wv8_plane", align_bytes=64)
 
         def fp4_weight(i, t):
-            return w_words[i][:, 2 * P * t : 2 * P * (t + 1)].bitcast(FP4X4), w_plane[:, i, P * t : P * (t + 1)]
+            return w_words[i][:, 2 * P * t : 2 * P * (t + 1)].bitcast(FP4X4), w_planes[i][:, P * t : P * (t + 1)]
 
         def product(bank, weights, h):
             for a, (w, s) in enumerate(weights):

@@ -41,8 +41,8 @@ def tile_list_engram_qf_sigLP_kernel(
 
         tab_plane = held.tile([P, T], U8, name="tab_plane", align_bytes=64)
         nc.vector.memset(tab_plane[:].bitcast(I32), 0)
-        wk_plane_raw = held.tile([P, 2, N], U8, name="wk_plane_raw", tag="picked1", align_bytes=64)
-        nc.gpsimd.memset(wk_plane_raw[:].rearrange("p i n -> p (i n)").bitcast(I32), 0)
+        wk_plane_raw = held.tile([P, 2, N], U8, name="wk_plane_raw", align_bytes=64)
+        nc.vector.memset(wk_plane_raw[:].rearrange("p i n -> p (i n)").bitcast(I32), 0)
         wv4_plane_raw = held.tile([P, N], U8, name="wv4_plane_raw", align_bytes=64)
         nc.gpsimd.memset(wv4_plane_raw[:].bitcast(I32), 0)
 
@@ -51,21 +51,16 @@ def tile_list_engram_qf_sigLP_kernel(
 
         wk_raw = held.tile([P, 2, 2 * N], U8, name="wk_raw", align_bytes=64)
         nc.sync.dma_start(wk_raw[:].bitcast(I32), wk_words.rearrange("a p b -> p a b").bitcast(I32))
-        wv4_raw = held.tile([P, 2 * N], U8, name="wv4_raw", align_bytes=64)
-        nc.sync.dma_start(wv4_raw[:].bitcast(I32), wv4_words[0].bitcast(I32))
 
+        nc.sync.dma_start(tab_plane[4:20, :].bitcast(I32), tab_scales[1].bitcast(I32))
         for q in range(4):
             nc.sync.dma_start(
-                tab_plane[32 * q : 32 * q + 8, :].bitcast(I32),
-                tab_scales[:, 4 * q : 4 * q + 4, :].bitcast(I32),
+                tab_plane[32 * q : 32 * q + 4, :].bitcast(I32), tab_scales[0, 4 * q : 4 * q + 4, :].bitcast(I32)
             )
-        tab = held.tile([P, T], I32, name="tab", tag="big1", align_bytes=64)
-        nc.sync.dma_start(tab[:], tab_words[0].rearrange("p t b -> p (t b)").bitcast(I32))
-        wv8_raw = held.tile([P, PACK, N], F32, name="wv8_raw", tag="big2", align_bytes=64)
-        nc.sync.dma_start(wv8_raw[:], wv8.rearrange("(p i) n -> p i n", i=PACK))
-
+        wv4_raw = held.tile([P, 2 * N], U8, name="wv4_raw", align_bytes=64)
+        nc.sync.dma_start(wv4_raw[:].bitcast(I32), wv4_words[0].bitcast(I32))
         for q in range(4):
-            nc.gpsimd.dma_start(
+            nc.sync.dma_start(
                 wk_plane_raw[32 * q : 32 * q + 4, :, :].bitcast(I32),
                 wk_scales[:, 4 * q : 4 * q + 4, :].rearrange("a r n -> r a n").bitcast(I32),
             )
@@ -75,6 +70,8 @@ def tile_list_engram_qf_sigLP_kernel(
                 wv4_scales[0, 4 * q : 4 * q + 4, :].bitcast(I32),
             )
 
+        tab = held.tile([P, T], I32, name="tab", tag="big1", align_bytes=64)
+        nc.sync.dma_start(tab[:], tab_words[0].rearrange("p t b -> p (t b)").bitcast(I32))
         st_rows = st.rearrange("(p t) j -> p t j", t=PACK)
         r_rows = rT.rearrange("(p t) c -> p t c", t=PACK)
         y_rows = out_0.rearrange("(p t) j -> p t j", t=PACK)
@@ -82,8 +79,10 @@ def tile_list_engram_qf_sigLP_kernel(
             held.tile([P, PACK, HALF], F32, name="state%d" % h, tag=("big3", "big4")[h], align_bytes=64)
             for h in range(2)
         ]
-        for h in range(2):
-            nc.sync.dma_start(state[h][:], st_rows[:, :, h * HALF : (h + 1) * HALF])
+        nc.sync.dma_start(state[0][:], st_rows[:, :, 0:HALF])
+        wv8_raw = held.tile([P, PACK, N], F32, name="wv8_raw", tag="big2", align_bytes=64)
+        nc.sync.dma_start(wv8_raw[:], wv8.rearrange("(p i) n -> p i n", i=PACK))
+        nc.sync.dma_start(state[1][:], st_rows[:, :, HALF:J])
         record = []
 
         def load_record(t):
@@ -96,6 +95,14 @@ def tile_list_engram_qf_sigLP_kernel(
             wk_w[:].bitcast(U16).rearrange("p a (t m) -> p a t m", t=PACK),
             wk_raw[:].bitcast(U16).rearrange("p a (m t) -> p a t m", t=PACK),
         )
+
+        nc.vector.tensor_copy(v_plane[0][:], tab_plane[:].indirect(offsets[:]))
+        for q in range(4):
+            nc.scalar.dma_start(
+                v_plane[1][32 * q : 32 * q + 4, :].bitcast(I32), v_plane[0][4 * q + 4 : 4 * q + 8, :].bitcast(I32)
+            )
+
+        load_record(0)
         wv4_w = held.tile([P, 2 * N], U8, name="wv4_w", align_bytes=64)
         nc.vector.tensor_copy(
             wv4_w[:].bitcast(U16).rearrange("p (t m) -> p t m", t=PACK),
@@ -103,26 +110,19 @@ def tile_list_engram_qf_sigLP_kernel(
         )
         w_words = (wk_w[:, 0, :], wk_w[:, 1, :], wv4_w[:])
 
-        nc.vector.tensor_copy(v_plane[0][:], tab_plane[:].indirect(offsets[:]))
-        for q in range(4):
-            nc.scalar.dma_start(
-                v_plane[1][32 * q : 32 * q + 4, :].bitcast(I32), v_plane[0][32 * q + 4 : 32 * q + 8, :].bitcast(I32)
-            )
-
-        load_record(0)
+        wk_plane = held.tile([P, 2, N], U8, name="wk_plane", align_bytes=64)
+        nc.vector.tensor_copy(
+            wk_plane[:].rearrange("p a (t m) -> p a t m", t=PACK),
+            wk_plane_raw[:].rearrange("p a (m t) -> p a t m", t=PACK),
+        )
         def pick_words(h):
-            picked = held.tile([P, HALF], U32, name="picked%d" % h, tag="picked%d" % h, align_bytes=64)
+            picked = held.tile([P, HALF], U32, name="picked%d" % h, align_bytes=64)
             nc.vector.tensor_copy(picked[:], tab[:].bitcast(U32).indirect(listed(h * HALF, HALF)))
             parted = held.tile([P, 2, 2 * HALF], U8, name="v_words%d" % h, align_bytes=64)
             nc.vector.tensor_copy(parted[:].bitcast(U16), picked[:].bitcast(U16).rearrange("p (j d) -> p d j", d=2))
             return parted
 
         v_words = [pick_words(0)]
-        wk_plane = held.tile([P, 2, N], U8, name="wk_plane", tag="picked0", align_bytes=64)
-        nc.vector.tensor_copy(
-            wk_plane[:].rearrange("p a (t m) -> p a t m", t=PACK),
-            wk_plane_raw[:].rearrange("p a (m t) -> p a t m", t=PACK),
-        )
         v_words.append(pick_words(1))
         wv4_plane = held.tile([P, N], U8, name="wv4_plane", align_bytes=64)
         nc.gpsimd.tensor_copy(
@@ -134,8 +134,8 @@ def tile_list_engram_qf_sigLP_kernel(
         load_record(1)
         wv8_b = held.tile([P, PACK * N], BF16, name="wv8_b", align_bytes=64)
         nc.scalar.copy(
-            wv8_b[:].rearrange("p (t m i) -> p m t i", t=PACK, i=PACK),
-            wv8_raw[:].rearrange("p i (m t) -> p m t i", t=PACK),
+            wv8_b[:].rearrange("p (u e m i) -> p u m i e", u=2, e=2, i=PACK),
+            wv8_raw[:].rearrange("p i (m u e) -> p u m i e", u=2, e=2),
         )
         load_record(2)
         wv8_codes = held.tile([P, N], U32, name="wv8_codes", align_bytes=64)
@@ -156,7 +156,7 @@ def tile_list_engram_qf_sigLP_kernel(
                     stop=(a == 1),
                 )
 
-        gated = [held.tile([P, J], F32, name="gated%d" % t) for t in range(PACK)]
+        gated = {}
 
         def gates(h):
             out = []
@@ -175,7 +175,13 @@ def tile_list_engram_qf_sigLP_kernel(
                 ve = psum.tile([P, HALF], F32, name="ve%d" % t)
                 w8 = (wv8_codes[:, P * t : P * (t + 1)].bitcast(FP8X4), wv8_plane[:, P * t : P * (t + 1)])
                 product(ve, (w8, fp4_weight(2, t)), h)
-                nc.vector.tensor_tensor(gated[t][:, h * HALF : (h + 1) * HALF], ve[:], gate[t][:], MULT)
+                width = HALF if t < PACK - 1 else HALF // 2
+                for c0 in range(0, HALF, width):
+                    j0 = h * HALF + c0
+                    m = held.tile([P, width], F32, name="gated", tag="gated%d_%d" % (t, j0))
+                    nc.vector.tensor_tensor(m[:], ve[:, c0 : c0 + width], gate[t][:, c0 : c0 + width], MULT)
+                    for c in range(0, width, P):
+                        gated[(t, j0 + c)] = (m, c)
 
         y_plane = held.tile([P, J], U8, name="y_plane", align_bytes=64)
         y_codes = held.tile([P, J], U32, name="y_codes", align_bytes=64)
@@ -188,39 +194,36 @@ def tile_list_engram_qf_sigLP_kernel(
         values(0, gate0)
         values(1, gate1)
 
-        rounded = [held.tile([P, width, PACK], BF16, name="yb%d" % j0, align_bytes=64) for j0, width in PIECES]
-        y01 = held.tile([P, 2, J], F32, name="y01")
-        for t in range(2):
-            nc.vector.tensor_tensor(y01[:, t, :], record[t][:].indirect(offsets[:]), gated[t][:], ADD)
-            nc.sync.dma_start(y_rows[:, t, :], y01[:, t, :])
-        for (j0, width), yb in zip(PIECES, rounded):
-            nc.scalar.copy(yb[:, :, 0:2], y01[:, :, j0 : j0 + width].rearrange("p t j -> p j t"))
+        def add_records(i):
+            j0, width = PIECES[i]
+            tag = "y%d" % j0 if i < 2 else "gated%d_%d" % (PACK - 1, PIECES[i - 2][0])
+            y = held.tile([P, PACK, width], F32, name="y", tag=tag)
+            for t in range(PACK):
+                m, c = gated[(t, j0)]
+                nc.vector.tensor_tensor(y[:, t, :], record[t][:].indirect(listed(j0, width)), m[:, c : c + width], ADD)
+            nc.sync.dma_start(y_rows[:, :, j0 : j0 + width], y[:])
+            yb = held.tile([P, width * PACK], BF16, name="yb%d" % j0, align_bytes=64)
+            nc.scalar.copy(
+                yb[:].rearrange("p (c e t) -> p c t e", e=2, t=PACK), y[:].rearrange("p t (c e) -> p c t e", e=2)
+            )
+            return yb
 
-        def add_records(j0, width, yb):
-            y23 = held.tile([P, 2, width], F32, name="y23_%d" % j0)
-            for t in (2, 3):
-                nc.vector.tensor_tensor(
-                    y23[:, t - 2, :], record[t][:].indirect(listed(j0, width)), gated[t][:, j0 : j0 + width], ADD
-                )
-            nc.sync.dma_start(y_rows[:, 2:4, j0 : j0 + width], y23[:])
-            nc.scalar.copy(yb[:, :, 2:4], y23[:].rearrange("p t j -> p j t"))
-
-        def quantise(j0, width, yb):
+        def quantise(i, yb):
+            j0, width = PIECES[i]
             nc.vector.quantize_mx(
-                out=y_codes[:, j0 : j0 + width].bitcast(FP8X4),
-                scales=y_plane[:, j0 : j0 + width],
-                in_=yb[:].rearrange("p j t -> p (j t)"),
+                out=y_codes[:, j0 : j0 + width].bitcast(FP8X4), scales=y_plane[:, j0 : j0 + width], in_=yb[:]
             )
 
-        for i, (j0, width) in enumerate(PIECES):
-            add_records(j0, width, rounded[i])
+        rounded = []
+        for i in range(len(PIECES)):
+            rounded.append(add_records(i))
             if i > 0:
-                quantise(*PIECES[i - 1], rounded[i - 1])
+                quantise(i - 1, rounded[i - 1])
             if i == 3:
-                nc.sync.dma_start(out_words[:, 0:j0], y_codes[:, 0:j0].bitcast(I32))
-        quantise(*PIECES[-1], rounded[-1])
+                nc.sync.dma_start(out_words[:, 0 : PIECES[3][0]], y_codes[:, 0 : PIECES[3][0]].bitcast(I32))
+        quantise(len(PIECES) - 1, rounded[-1])
         nc.sync.dma_start(out_words[:, PIECES[3][0] : J], y_codes[:, PIECES[3][0] : J].bitcast(I32))
         for q in range(4):
-            nc.scalar.dma_start(
+            (nc.scalar, nc.sync)[q // 2].dma_start(
                 out_2[0, 4 * q : 4 * q + 4, :].bitcast(I32), y_plane[32 * q : 32 * q + 4, :].bitcast(I32)
             )

@@ -39,9 +39,9 @@ def tile_list_engram_qf_sigLP_kernel(
         def listed(j0, width):
             return offsets[:, j0 // LIST_ROWS : (j0 + width) // LIST_ROWS]
 
-        tab_plane = held.tile([P, T], U8, name="tab_plane", align_bytes=64)
+        tab_plane = held.tile([P, T], U8, name="tab_plane", tag="state0", align_bytes=64)
         nc.vector.memset(tab_plane[:].bitcast(I32), 0)
-        wk_plane_raw = held.tile([P, 2, N], U8, name="wk_plane_raw", align_bytes=64)
+        wk_plane_raw = held.tile([P, 2, N], U8, name="wk_plane_raw", tag="state1", align_bytes=64)
         nc.vector.memset(wk_plane_raw[:].rearrange("p i n -> p (i n)").bitcast(I32), 0)
         wv4_plane_raw = held.tile([P, N], U8, name="wv4_plane_raw", align_bytes=64)
         nc.gpsimd.memset(wv4_plane_raw[:].bitcast(I32), 0)
@@ -51,14 +51,16 @@ def tile_list_engram_qf_sigLP_kernel(
 
         wk_raw = held.tile([P, 2, 2 * N], U8, name="wk_raw", align_bytes=64)
         nc.sync.dma_start(wk_raw[:].bitcast(I32), wk_words.rearrange("a p b -> p a b").bitcast(I32))
+        wv4_raw = held.tile([P, 2 * N], U8, name="wv4_raw", align_bytes=64)
+        nc.sync.dma_start(wv4_raw[:].bitcast(I32), wv4_words[0].bitcast(I32))
 
         nc.sync.dma_start(tab_plane[4:20, :].bitcast(I32), tab_scales[1].bitcast(I32))
         for q in range(4):
             nc.sync.dma_start(
                 tab_plane[32 * q : 32 * q + 4, :].bitcast(I32), tab_scales[0, 4 * q : 4 * q + 4, :].bitcast(I32)
             )
-        wv4_raw = held.tile([P, 2 * N], U8, name="wv4_raw", align_bytes=64)
-        nc.sync.dma_start(wv4_raw[:].bitcast(I32), wv4_words[0].bitcast(I32))
+        tab = held.tile([P, T], I32, name="tab", tag="big0", align_bytes=64)
+        nc.sync.dma_start(tab[:], tab_words[0].rearrange("p t b -> p (t b)").bitcast(I32))
         for q in range(4):
             nc.sync.dma_start(
                 wk_plane_raw[32 * q : 32 * q + 4, :, :].bitcast(I32),
@@ -70,19 +72,29 @@ def tile_list_engram_qf_sigLP_kernel(
                 wv4_scales[0, 4 * q : 4 * q + 4, :].bitcast(I32),
             )
 
-        tab = held.tile([P, T], I32, name="tab", tag="big1", align_bytes=64)
-        nc.sync.dma_start(tab[:], tab_words[0].rearrange("p t b -> p (t b)").bitcast(I32))
+        wv8_raw = held.tile([P, PACK, N], F32, name="wv8_raw", tag="big3", align_bytes=64)
+        nc.sync.dma_start(wv8_raw[:], wv8.rearrange("(p i) n -> p i n", i=PACK))
+        wk_w = held.tile([P, 2, 2 * N], U8, name="wk_w", align_bytes=64)
+        nc.vector.tensor_copy(
+            wk_w[:].bitcast(U16).rearrange("p a (t m) -> p a t m", t=PACK),
+            wk_raw[:].bitcast(U16).rearrange("p a (m t) -> p a t m", t=PACK),
+        )
+        nc.vector.tensor_copy(v_plane[0][:], tab_plane[:].indirect(offsets[:]))
+        for q in range(4):
+            nc.sync.dma_start(
+                v_plane[1][32 * q : 32 * q + 4, :].bitcast(I32), v_plane[0][4 * q + 4 : 4 * q + 8, :].bitcast(I32)
+            )
         st_rows = st.rearrange("(p t) j -> p t j", t=PACK)
         r_rows = rT.rearrange("(p t) c -> p t c", t=PACK)
         y_rows = out_0.rearrange("(p t) j -> p t j", t=PACK)
-        state = [
-            held.tile([P, PACK, HALF], F32, name="state%d" % h, tag=("big3", "big4")[h], align_bytes=64)
-            for h in range(2)
-        ]
-        nc.sync.dma_start(state[0][:], st_rows[:, :, 0:HALF])
-        wv8_raw = held.tile([P, PACK, N], F32, name="wv8_raw", tag="big2", align_bytes=64)
-        nc.sync.dma_start(wv8_raw[:], wv8.rearrange("(p i) n -> p i n", i=PACK))
-        nc.sync.dma_start(state[1][:], st_rows[:, :, HALF:J])
+        state = []
+
+        def load_state(h):
+            s = held.tile([P, PACK, HALF], F32, name="state%d" % h, tag="state%d" % h, align_bytes=64)
+            nc.sync.dma_start(s[:], st_rows[:, :, h * HALF : (h + 1) * HALF])
+            state.append(s)
+
+        load_state(0)
         record = []
 
         def load_record(t):
@@ -90,19 +102,6 @@ def tile_list_engram_qf_sigLP_kernel(
             nc.sync.dma_start(r[:], r_rows[:, t, :])
             record.append(r)
 
-        wk_w = held.tile([P, 2, 2 * N], U8, name="wk_w", align_bytes=64)
-        nc.vector.tensor_copy(
-            wk_w[:].bitcast(U16).rearrange("p a (t m) -> p a t m", t=PACK),
-            wk_raw[:].bitcast(U16).rearrange("p a (m t) -> p a t m", t=PACK),
-        )
-
-        nc.vector.tensor_copy(v_plane[0][:], tab_plane[:].indirect(offsets[:]))
-        for q in range(4):
-            nc.scalar.dma_start(
-                v_plane[1][32 * q : 32 * q + 4, :].bitcast(I32), v_plane[0][4 * q + 4 : 4 * q + 8, :].bitcast(I32)
-            )
-
-        load_record(0)
         wv4_w = held.tile([P, 2 * N], U8, name="wv4_w", align_bytes=64)
         nc.vector.tensor_copy(
             wv4_w[:].bitcast(U16).rearrange("p (t m) -> p t m", t=PACK),
@@ -115,8 +114,10 @@ def tile_list_engram_qf_sigLP_kernel(
             wk_plane[:].rearrange("p a (t m) -> p a t m", t=PACK),
             wk_plane_raw[:].rearrange("p a (m t) -> p a t m", t=PACK),
         )
+        load_state(1)
+
         def pick_words(h):
-            picked = held.tile([P, HALF], U32, name="picked%d" % h, align_bytes=64)
+            picked = held.tile([P, HALF], U32, name="picked%d" % h, tag="big%d" % (1 + h), align_bytes=64)
             nc.vector.tensor_copy(picked[:], tab[:].bitcast(U32).indirect(listed(h * HALF, HALF)))
             parted = held.tile([P, 2, 2 * HALF], U8, name="v_words%d" % h, align_bytes=64)
             nc.vector.tensor_copy(parted[:].bitcast(U16), picked[:].bitcast(U16).rearrange("p (j d) -> p d j", d=2))
@@ -124,6 +125,9 @@ def tile_list_engram_qf_sigLP_kernel(
 
         v_words = [pick_words(0)]
         v_words.append(pick_words(1))
+        load_record(0)
+        load_record(1)
+        load_record(2)
         wv4_plane = held.tile([P, N], U8, name="wv4_plane", align_bytes=64)
         nc.gpsimd.tensor_copy(
             wv4_plane[:].rearrange("p (t m) -> p t m", t=PACK),
@@ -131,13 +135,15 @@ def tile_list_engram_qf_sigLP_kernel(
         )
         w_planes = (wk_plane[:, 0, :], wk_plane[:, 1, :], wv4_plane[:])
 
-        load_record(1)
-        wv8_b = held.tile([P, PACK * N], BF16, name="wv8_b", align_bytes=64)
-        nc.scalar.copy(
-            wv8_b[:].rearrange("p (u e m i) -> p u m i e", u=2, e=2, i=PACK),
-            wv8_raw[:].rearrange("p i (m u e) -> p u m i e", u=2, e=2),
-        )
-        load_record(2)
+        wv8_b = []
+        for u in range(2):
+            b = held.tile([P, 2 * N], BF16, name="wv8_b", tag="wv8_b%d" % u, align_bytes=64)
+            nc.scalar.copy(
+                b[:].rearrange("p (e m i) -> p m i e", e=2, i=PACK),
+                wv8_raw[:].rearrange("p i (m u e) -> p u m i e", u=2, e=2)[:, u],
+            )
+            wv8_b.append(b)
+        load_record(3)
         wv8_codes = held.tile([P, N], U32, name="wv8_codes", align_bytes=64)
         wv8_plane = held.tile([P, N], U8, name="wv8_plane", align_bytes=64)
 
@@ -145,58 +151,77 @@ def tile_list_engram_qf_sigLP_kernel(
             return w_words[i][:, 2 * P * t : 2 * P * (t + 1)].bitcast(FP4X4), w_planes[i][:, P * t : P * (t + 1)]
 
         def product(bank, weights, h):
-            for a, (w, s) in enumerate(weights):
+            for a in (1, 0):
+                w, s = weights[a]
                 nc.tensor.matmul_mx(
                     out=bank[:],
                     lhsT=w,
                     lhsT_scale=s,
                     rhs=v_words[h][:, a, :].bitcast(FP4X4),
                     rhs_scale=v_plane[a][:, h * HALF : (h + 1) * HALF],
-                    start=(a == 0),
-                    stop=(a == 1),
+                    start=(a == 1),
+                    stop=(a == 0),
                 )
 
         gated = {}
 
-        def gates(h):
-            out = []
-            for t in range(PACK):
-                ke = psum.tile([P, HALF], F32, name="ke%d" % t)
-                product(ke, (fp4_weight(0, t), fp4_weight(1, t)), h)
-                z = ring.tile([P, HALF], F32, name="z")
-                nc.vector.tensor_tensor(z[:], ke[:], state[h][:, t, :], MULT)
-                gate = ring.tile([P, HALF], F32, name="gate")
-                nc.scalar.activation(gate[:], z[:], SIGMOID)
-                out.append(gate)
-            return out
+        def key(h, t):
+            ke = psum.tile([P, HALF], F32, name="ke%d" % t)
+            product(ke, (fp4_weight(0, t), fp4_weight(1, t)), h)
+            return ke
 
-        def values(h, gate):
-            for t in range(PACK):
-                ve = psum.tile([P, HALF], F32, name="ve%d" % t)
-                w8 = (wv8_codes[:, P * t : P * (t + 1)].bitcast(FP8X4), wv8_plane[:, P * t : P * (t + 1)])
-                product(ve, (w8, fp4_weight(2, t)), h)
-                width = HALF if t < PACK - 1 else HALF // 2
-                for c0 in range(0, HALF, width):
-                    j0 = h * HALF + c0
-                    m = held.tile([P, width], F32, name="gated", tag="gated%d_%d" % (t, j0))
-                    nc.vector.tensor_tensor(m[:], ve[:, c0 : c0 + width], gate[t][:, c0 : c0 + width], MULT)
-                    for c in range(0, width, P):
-                        gated[(t, j0 + c)] = (m, c)
+        def logit_on_vector(h, t):
+            z = late_logits[:, t * HALF : (t + 1) * HALF] if h == 1 else ring.tile([P, HALF], F32, name="z")[:]
+            nc.vector.tensor_tensor(z, key(h, t)[:], state[h][:, t, :], MULT)
+            return z
+
+        def logit_on_gpsimd(h, t):
+            ke = key_rows[:, (t - 2) * HALF : (t - 1) * HALF]
+            nc.scalar.copy(ke, key(h, t)[:])
+            z = ring.tile([P, HALF], F32, name="z")
+            nc.gpsimd.tensor_tensor(z[:], ke, state[h][:, t, :], MULT)
+            return z[:]
+
+        def gated_value(h, t, z):
+            ve = psum.tile([P, HALF], F32, name="ve%d" % t)
+            w8 = (wv8_codes[:, P * t : P * (t + 1)].bitcast(FP8X4), wv8_plane[:, P * t : P * (t + 1)])
+            width = HALF if t < PACK - 1 else HALF // 2
+            gates = []
+            for c0 in range(0, HALF, width):
+                gate = held.tile([P, width], F32, name="gate", tag="gate%d_%d" % (t, h * HALF + c0))
+                nc.scalar.activation(gate[:], z[:, c0 : c0 + width], SIGMOID)
+                gates.append(gate)
+            product(ve, (w8, fp4_weight(2, t)), h)
+            for c0 in range(0, HALF, width):
+                j0 = h * HALF + c0
+                m = held.tile([P, width], F32, name="gated", tag="gated%d_%d" % (t, j0))
+                nc.vector.tensor_tensor(m[:], ve[:, c0 : c0 + width], gates[c0 // width][:], MULT)
+                for c in range(0, width, P):
+                    gated[(t, j0 + c)] = (m, c)
 
         y_plane = held.tile([P, J], U8, name="y_plane", align_bytes=64)
         y_codes = held.tile([P, J], U32, name="y_codes", align_bytes=64)
         out_words = out_1[0].rearrange("p j b -> p (j b)").bitcast(I32)
 
-        gate0 = gates(0)
-        load_record(3)
-        nc.vector.quantize_mx(out=wv8_codes[:].bitcast(FP8X4), scales=wv8_plane[:], in_=wv8_b[:])
-        gate1 = gates(1)
-        values(0, gate0)
-        values(1, gate1)
+        for u in range(2):
+            cols = slice(u * N // 2, (u + 1) * N // 2)
+            nc.vector.quantize_mx(out=wv8_codes[:, cols].bitcast(FP8X4), scales=wv8_plane[:, cols], in_=wv8_b[u][:])
+        key_rows = held.tile([P, 2 * HALF], F32, name="key_rows", tag="wv8_b1", align_bytes=64)
+        late_logits = held.tile([P, 2 * HALF], F32, name="late_logits", tag="wv8_b0", align_bytes=64)
+        logit = {}
+        for t in range(PACK):
+            logit[(0, t)] = logit_on_vector(0, t)
+        for t in (2, 3):
+            logit[(1, t)] = logit_on_gpsimd(1, t)
+        for t in (0, 1):
+            logit[(1, t)] = logit_on_vector(1, t)
+        for h in range(2):
+            for t in range(PACK):
+                gated_value(h, t, logit[(h, t)])
 
         def add_records(i):
             j0, width = PIECES[i]
-            tag = "y%d" % j0 if i < 2 else "gated%d_%d" % (PACK - 1, PIECES[i - 2][0])
+            tag = "gate%d_%d" % (PACK - 1, HALF + j0) if i < 2 else "gated%d_%d" % (PACK - 1, PIECES[i - 2][0])
             y = held.tile([P, PACK, width], F32, name="y", tag=tag)
             for t in range(PACK):
                 m, c = gated[(t, j0)]

from contextlib import ExitStack

import concourse.mybir as mybir

K, N, T, J = 1024, 512, 2048, 1024
FLOPS = 2 * 2 * K * N * J

F32 = mybir.dt.float32
BF16 = mybir.dt.bfloat16
I32 = mybir.dt.int32
U32 = mybir.dt.uint32
U16 = mybir.dt.uint16
U8 = mybir.dt.uint8
FP8X4 = mybir.dt.float8_e4m3fn_x4
FP4X4 = mybir.dt.float4_e2m1fn_x4
MULT = mybir.AluOpType.mult
ADD = mybir.AluOpType.add
SIGMOID = mybir.ActivationFunctionType.Sigmoid

P = 128
PACK = 4
HALF = 512
LIST_ROWS = 16
PIECES = ((0, 256), (256, 256), (512, 256), (768, 128), (896, 128))


def tile_list_engram_qf_sigLP_kernel(
    tc, tab_words, tab_scales, wk_words, wk_scales, wv8, wv4_words, wv4_scales, st, rT, offs, out_0, out_1, out_2
):
    nc = tc.nc
    with ExitStack() as ctx:
        held = ctx.enter_context(tc.tile_pool(name="held", bufs=1))
        ring = ctx.enter_context(tc.tile_pool(name="ring", bufs=8))
        psum = ctx.enter_context(tc.psum_pool(name="psum", bufs=1))

        offsets = held.tile([P, J // LIST_ROWS], U16, name="offsets")
        nc.sync.dma_start(offsets[:], offs)

        def listed(j0, width):
            return offsets[:, j0 // LIST_ROWS : (j0 + width) // LIST_ROWS]

        tab_plane = held.tile([P, T], U8, name="tab_plane", tag="state0", align_bytes=64)
        nc.vector.memset(tab_plane[:].bitcast(I32), 0)
        wk_plane_raw = held.tile([P, 2, N], U8, name="wk_plane_raw", tag="state1", align_bytes=64)
        nc.vector.memset(wk_plane_raw[:].rearrange("p i n -> p (i n)").bitcast(I32), 0)
        wv4_plane_raw = held.tile([P, N], U8, name="wv4_plane_raw", align_bytes=64)
        nc.gpsimd.memset(wv4_plane_raw[:].bitcast(I32), 0)

        v_plane = [held.tile([P, J], U8, name="v_plane%d" % a, align_bytes=64) for a in range(2)]
        nc.gpsimd.memset(v_plane[1][:].bitcast(I32), 0)

        wk_raw = held.tile([P, 2, 2 * N], U8, name="wk_raw", align_bytes=64)
        nc.sync.dma_start(wk_raw[:].bitcast(I32), wk_words.rearrange("a p b -> p a b").bitcast(I32))
        wv4_raw = held.tile([P, 2 * N], U8, name="wv4_raw", align_bytes=64)
        nc.sync.dma_start(wv4_raw[:].bitcast(I32), wv4_words[0].bitcast(I32))

        nc.sync.dma_start(tab_plane[4:20, :].bitcast(I32), tab_scales[1].bitcast(I32))
        for q in range(4):
            nc.sync.dma_start(
                tab_plane[32 * q : 32 * q + 4, :].bitcast(I32), tab_scales[0, 4 * q : 4 * q + 4, :].bitcast(I32)
            )
        tab = held.tile([P, T], I32, name="tab", tag="big0", align_bytes=64)
        nc.sync.dma_start(tab[:], tab_words[0].rearrange("p t b -> p (t b)").bitcast(I32))
        for q in range(4):
            nc.sync.dma_start(
                wk_plane_raw[32 * q : 32 * q + 4, :, :].bitcast(I32),
                wk_scales[:, 4 * q : 4 * q + 4, :].rearrange("a r n -> r a n").bitcast(I32),
            )
        for q in range(4):
            nc.gpsimd.dma_start(
                wv4_plane_raw[32 * q : 32 * q + 4, :].bitcast(I32),
                wv4_scales[0, 4 * q : 4 * q + 4, :].bitcast(I32),
            )

        wv8_raw = held.tile([P, PACK, N], F32, name="wv8_raw", tag="big3", align_bytes=64)
        nc.sync.dma_start(wv8_raw[:], wv8.rearrange("(p i) n -> p i n", i=PACK))
        wk_w = held.tile([P, 2, 2 * N], U8, name="wk_w", align_bytes=64)
        nc.vector.tensor_copy(
            wk_w[:].bitcast(U16).rearrange("p a (t m) -> p a t m", t=PACK),
            wk_raw[:].bitcast(U16).rearrange("p a (m t) -> p a t m", t=PACK),
        )
        nc.vector.tensor_copy(v_plane[0][:], tab_plane[:].indirect(offsets[:]))
        for q in range(4):
            nc.sync.dma_start(
                v_plane[1][32 * q : 32 * q + 4, :].bitcast(I32), v_plane[0][4 * q + 4 : 4 * q + 8, :].bitcast(I32)
            )
        st_rows = st.rearrange("(p t) j -> p t j", t=PACK)
        r_rows = rT.rearrange("(p t) c -> p t c", t=PACK)
        y_rows = out_0.rearrange("(p t) j -> p t j", t=PACK)
        state = []

        def load_state(h):
            s = held.tile([P, PACK, HALF], F32, name="state%d" % h, tag="state%d" % h, align_bytes=64)
            nc.sync.dma_start(s[:], st_rows[:, :, h * HALF : (h + 1) * HALF])
            state.append(s)

        load_state(0)
        record = []

        def load_record(t):
            r = held.tile([P, T], F32, name="record%d" % t, tag="big%d" % t, align_bytes=64)
            nc.sync.dma_start(r[:], r_rows[:, t, :])
            record.append(r)

        wv4_w = held.tile([P, 2 * N], U8, name="wv4_w", align_bytes=64)
        nc.vector.tensor_copy(
            wv4_w[:].bitcast(U16).rearrange("p (t m) -> p t m", t=PACK),
            wv4_raw[:].bitcast(U16).rearrange("p (m t) -> p t m", t=PACK),
        )
        w_words = (wk_w[:, 0, :], wk_w[:, 1, :], wv4_w[:])

        wk_plane = held.tile([P, 2, N], U8, name="wk_plane", align_bytes=64)
        nc.vector.tensor_copy(
            wk_plane[:].rearrange("p a (t m) -> p a t m", t=PACK),
            wk_plane_raw[:].rearrange("p a (m t) -> p a t m", t=PACK),
        )
        load_state(1)

        def pick_words(h):
            picked = held.tile([P, HALF], U32, name="picked%d" % h, tag="big%d" % (1 + h), align_bytes=64)
            nc.vector.tensor_copy(picked[:], tab[:].bitcast(U32).indirect(listed(h * HALF, HALF)))
            parted = held.tile([P, 2, 2 * HALF], U8, name="v_words%d" % h, align_bytes=64)
            nc.vector.tensor_copy(parted[:].bitcast(U16), picked[:].bitcast(U16).rearrange("p (j d) -> p d j", d=2))
            return parted

        v_words = [pick_words(0)]
        v_words.append(pick_words(1))
        load_record(0)
        load_record(1)
        load_record(2)
        wv4_plane = held.tile([P, N], U8, name="wv4_plane", align_bytes=64)
        nc.gpsimd.tensor_copy(
            wv4_plane[:].rearrange("p (t m) -> p t m", t=PACK),
            wv4_plane_raw[:].rearrange("p (m t) -> p t m", t=PACK),
        )
        w_planes = (wk_plane[:, 0, :], wk_plane[:, 1, :], wv4_plane[:])

        wv8_b = []
        for u in range(2):
            b = held.tile([P, 2 * N], BF16, name="wv8_b", tag="wv8_b%d" % u, align_bytes=64)
            nc.scalar.copy(
                b[:].rearrange("p (e m i) -> p m i e", e=2, i=PACK),
                wv8_raw[:].rearrange("p i (m u e) -> p u m i e", u=2, e=2)[:, u],
            )
            wv8_b.append(b)
        load_record(3)
        wv8_codes = held.tile([P, N], U32, name="wv8_codes", align_bytes=64)
        wv8_plane = held.tile([P, N], U8, name="wv8_plane", align_bytes=64)

        def fp4_weight(i, t):
            return w_words[i][:, 2 * P * t : 2 * P * (t + 1)].bitcast(FP4X4), w_planes[i][:, P * t : P * (t + 1)]

        def product(bank, weights, h):
            for a in (1, 0):
                w, s = weights[a]
                nc.tensor.matmul_mx(
                    out=bank[:],
                    lhsT=w,
                    lhsT_scale=s,
                    rhs=v_words[h][:, a, :].bitcast(FP4X4),
                    rhs_scale=v_plane[a][:, h * HALF : (h + 1) * HALF],
                    start=(a == 1),
                    stop=(a == 0),
                )

        gated = {}

        def key(h, t):
            ke = psum.tile([P, HALF], F32, name="ke%d" % t)
            product(ke, (fp4_weight(0, t), fp4_weight(1, t)), h)
            return ke

        def logit_on_vector(h, t):
            z = late_logits[:, t * HALF : (t + 1) * HALF] if h == 1 else ring.tile([P, HALF], F32, name="z")[:]
            nc.vector.tensor_tensor(z, key(h, t)[:], state[h][:, t, :], MULT)
            return z

        def logit_on_gpsimd(h, t):
            ke = key_rows[:, (t - 2) * HALF : (t - 1) * HALF]
            nc.scalar.copy(ke, key(h, t)[:])
            z = ring.tile([P, HALF], F32, name="z")
            nc.gpsimd.tensor_tensor(z[:], ke, state[h][:, t, :], MULT)
            return z[:]

        def gated_value(h, t, z):
            ve = psum.tile([P, HALF], F32, name="ve%d" % t)
            w8 = (wv8_codes[:, P * t : P * (t + 1)].bitcast(FP8X4), wv8_plane[:, P * t : P * (t + 1)])
            width = HALF if t < PACK - 1 else HALF // 2
            gates = []
            for c0 in range(0, HALF, width):
                gate = held.tile([P, width], F32, name="gate", tag="gate%d_%d" % (t, h * HALF + c0))
                nc.scalar.activation(gate[:], z[:, c0 : c0 + width], SIGMOID)
                gates.append(gate)
            product(ve, (w8, fp4_weight(2, t)), h)
            for c0 in range(0, HALF, width):
                j0 = h * HALF + c0
                m = held.tile([P, width], F32, name="gated", tag="gated%d_%d" % (t, j0))
                nc.vector.tensor_tensor(m[:], ve[:, c0 : c0 + width], gates[c0 // width][:], MULT)
                for c in range(0, width, P):
                    gated[(t, j0 + c)] = (m, c)

        y_plane = held.tile([P, J], U8, name="y_plane", align_bytes=64)
        y_codes = held.tile([P, J], U32, name="y_codes", align_bytes=64)
        out_words = out_1[0].rearrange("p j b -> p (j b)").bitcast(I32)

        for u in range(2):
            cols = slice(u * N // 2, (u + 1) * N // 2)
            nc.vector.quantize_mx(out=wv8_codes[:, cols].bitcast(FP8X4), scales=wv8_plane[:, cols], in_=wv8_b[u][:])
        key_rows = held.tile([P, 2 * HALF], F32, name="key_rows", tag="wv8_b1", align_bytes=64)
        late_logits = held.tile([P, 2 * HALF], F32, name="late_logits", tag="wv8_b0", align_bytes=64)
        logit = {}
        for t in range(PACK):
            logit[(0, t)] = logit_on_vector(0, t)
        for t in (2, 3):
            logit[(1, t)] = logit_on_gpsimd(1, t)
        for t in (0, 1):
            logit[(1, t)] = logit_on_vector(1, t)
        for h in range(2):
            for t in range(PACK):
                gated_value(h, t, logit[(h, t)])

        def add_records(i):
            j0, width = PIECES[i]
            tag = "gate%d_%d" % (PACK - 1, HALF + j0) if i < 2 else "gated%d_%d" % (PACK - 1, PIECES[i - 2][0])
            y = held.tile([P, PACK, width], F32, name="y", tag=tag)
            for t in range(PACK):
                m, c = gated[(t, j0)]
                nc.vector.tensor_tensor(y[:, t, :], record[t][:].indirect(listed(j0, width)), m[:, c : c + width], ADD)
            nc.sync.dma_start(y_rows[:, :, j0 : j0 + width], y[:])
            yb = held.tile([P, width * PACK], BF16, name="yb%d" % j0, align_bytes=64)
            nc.scalar.copy(
                yb[:].rearrange("p (c e t) -> p c t e", e=2, t=PACK), y[:].rearrange("p t (c e) -> p c t e", e=2)
            )
            return yb

        def quantise(i, yb):
            j0, width = PIECES[i]
            nc.vector.quantize_mx(
                out=y_codes[:, j0 : j0 + width].bitcast(FP8X4), scales=y_plane[:, j0 : j0 + width], in_=yb[:]
            )

        rounded = []
        for i in range(len(PIECES)):
            rounded.append(add_records(i))
            if i > 0:
                quantise(i - 1, rounded[i - 1])
            if i == 3:
                nc.sync.dma_start(out_words[:, 0 : PIECES[3][0]], y_codes[:, 0 : PIECES[3][0]].bitcast(I32))
        quantise(len(PIECES) - 1, rounded[-1])
        nc.sync.dma_start(out_words[:, PIECES[3][0] : J], y_codes[:, PIECES[3][0] : J].bitcast(I32))
        for q in range(4):
            (nc.scalar, nc.sync)[q // 2].dma_start(
                out_2[0, 4 * q : 4 * q + 4, :].bitcast(I32), y_plane[32 * q : 32 * q + 4, :].bitcast(I32)
            )
